import numpy as np
import ml_dtypes


def mxq(x, axis, fmt="e4m3"):
    dtype, down = {"e4m3": (ml_dtypes.float8_e4m3fn, 7), "e5m2": (ml_dtypes.float8_e5m2, 14)}[fmt]
    v = np.moveaxis(np.asarray(x, np.float32).astype(ml_dtypes.bfloat16).astype(np.float64), axis, -1)
    blocks = v.reshape(v.shape[:-1] + (-1, 32))
    amax = np.abs(blocks).max(-1, keepdims=True)
    byte = np.maximum(np.where(amax > 0, np.frexp(amax)[1] - 1 + 127, 0) - down, 1)
    scale = np.exp2(byte - 127.0)
    codes = (blocks / scale).astype(np.float32).astype(dtype).astype(np.float64)
    return np.moveaxis((codes * scale).reshape(v.shape), -1, axis)


WIDE = False


def mx_kscale(k):
    if not WIDE:
        return np.ones(k)
    levels = np.array([10, -10, 5, -5, 0])
    if k % 512:
        return np.exp2(np.random.permutation(np.resize(levels, k // 32))).repeat(32)
    a = np.empty((k // 512, 16))
    for p in range(k // 512):
        a[p, :8] = np.random.permutation(np.resize(levels, 8))
        for g in range(8):
            far = levels[np.abs(levels - a[p, g]) >= 10]
            a[p, g + 8] = far[np.random.randint(len(far))]
    return np.exp2(a.ravel()).repeat(32)


def f64(x):
    return np.asarray(x).astype(np.float64)


def striped(idx):
    return np.tile(idx.reshape(-1, 16).T, (8, 1)).astype(np.uint16)


def unstriped(offs):
    return offs[:16].T.reshape(-1).astype(np.int64)


def pack_weight(w):
    k, n = w.shape
    w = f64(np.asarray(w, np.float32).astype(ml_dtypes.bfloat16)).reshape(k // 32, 32, n)
    amax = np.abs(w).max(1)
    byte = np.clip(np.where(amax > 0, np.frexp(amax)[1] - 1 + 127 - 7, 1), 1, 254)
    scaled = (w * np.exp2(127.0 - byte)[:, None, :]).reshape(k, n).astype(np.float32)
    words = np.ascontiguousarray(scaled.reshape(k // 512, 128, 4, n).transpose(0, 1, 3, 2)).astype(ml_dtypes.float8_e4m3fn).view(np.uint8)
    return words, np.ascontiguousarray(byte.astype(np.uint8).reshape(k // 512, 16, n))


def unpack_weight(words, scales):
    g, p, n, _ = words.shape
    vals = np.ascontiguousarray(words).view(ml_dtypes.float8_e4m3fn).astype(np.float64) * np.repeat(np.exp2(scales.astype(np.float64) - 127.0), 8, axis=1)[..., None]
    return vals.transpose(0, 1, 3, 2).reshape(g * 512, n)


def relu(v):
    return np.maximum(v, 0.0)


K, T, S, N = 1024, 2048, 512, 256


def setup_inputs():
    n = np.random.standard_normal
    s = mx_kscale(K)[:, None]
    packed_xT = pack_weight(n((K, T)) * s)
    return {
        "x_words": packed_xT[0],
        "x_scales": packed_xT[1],
        "w1": (n((K, N)) / np.sqrt(K) / s).astype(np.float32),
        "dual": (np.random.uniform(-1.0, 1.0, (N, S))).astype(np.float32),
        "data": (n((N, S))).astype(np.float32),
        "offs": striped(np.random.permutation(T)[:S]),
    }


def reference(x_words, x_scales, w1, dual, data, offs):
    xq = unpack_weight(x_words, x_scales)[:, unstriped(offs)]
    y = mxq(f64(w1), 0, "e4m3").T @ xq
    p1 = f64(dual) + 0.4 * (np.pad(y, ((0, 0), (0, 1)))[:, 1:] - y)
    pc = p1 - relu(p1 - 1.0) + relu(-1.0 * p1 - 1.0)
    div = pc - (np.pad(pc, ((0, 0), (1, 0)))[:, :S])
    return (y + 0.4 * div + 0.8 * f64(data)) / 1.8

@@ -1,0 +1,171 @@
+from contextlib import ExitStack
+
+import concourse.mybir as mybir
+
+K, T, S, N = 1024, 2048, 512, 256
+FLOPS = 2 * K * S * N
+
+F32 = mybir.dt.float32
+BF16 = mybir.dt.bfloat16
+I32 = mybir.dt.int32
+U32 = mybir.dt.uint32
+U16 = mybir.dt.uint16
+U8 = mybir.dt.uint8
+FP8X4 = mybir.dt.float8_e4m3fn_x4
+ALU = mybir.AluOpType
+ACT = mybir.ActivationFunctionType
+
+P = 128
+PACK = 4
+PASSES = K // (P * PACK)
+ROW_TILES = N // P
+STEP = 0.4
+C_DIV = 0.4 / 1.8
+C_Y = 1.0 / 1.8
+C_DATA = 0.8 / 1.8
+PAD = 8
+H = S // 2
+
+
+def tile_picked_ytvpd_step_p_kernel(tc, x_words, x_scales, w1, dual, data, offs, out):
+    nc = tc.nc
+    with ExitStack() as ctx:
+        keep = ctx.enter_context(tc.tile_pool(name="keep", bufs=1))
+        psum = ctx.enter_context(tc.psum_pool(name="psum", bufs=1))
+
+        offsets = keep.tile([P, S // 16], U16, name="offsets")
+        nc.sync.dma_start(offsets[:], offs)
+
+        scale_table = keep.tile([P, T], U8, name="scale_table", align_bytes=64)
+        nc.gpsimd.memset(scale_table[:].bitcast(I32), 0)
+        zero = keep.tile([P, 1], F32, name="zero")
+        nc.vector.memset(zero[:], 0.0)
+
+        r = [keep.tile([P, PAD + S], F32, name="r%d" % b, align_bytes=64) for b in range(ROW_TILES)]
+        for b in range(ROW_TILES):
+            nc.scalar.activation(r[b][:, PAD - 1 : PAD], zero[:], ACT.Relu, bias=C_DIV, scale=1.0)
+
+        w_raw = [keep.tile([P, PACK, N], F32, name="w_raw%d" % o, align_bytes=64) for o in range(PASSES)]
+        for o in range(PASSES):
+            nc.sync.dma_start(w_raw[o][:], w1[512 * o : 512 * (o + 1), :].rearrange("(p j) n -> p j n", j=PACK))
+            if o == 0:
+                for q in range(4):
+                    nc.sync.dma_start(
+                        scale_table[32 * q : 32 * q + 4 * PASSES, :].bitcast(I32),
+                        x_scales[:, 4 * q : 4 * q + 4, :].bitcast(I32),
+                    )
+
+        word_table = [keep.tile([P, T], I32, name="word_table%d" % o, align_bytes=64) for o in range(PASSES)]
+        for o in range(PASSES):
+            nc.sync.dma_start(word_table[o][:], x_words[o].rearrange("p c r -> p (c r)").bitcast(I32))
+        dual_sb = [keep.tile([P, S], F32, name="dual%d" % b, align_bytes=64) for b in range(ROW_TILES)]
+        data_sb = [keep.tile([P, S], F32, name="data%d" % b, align_bytes=64) for b in range(ROW_TILES)]
+        for sb, src, b in ((data_sb, data, 0), (dual_sb, dual, 0), (dual_sb, dual, 1), (data_sb, data, 1)):
+            nc.sync.dma_start(sb[b][:], src[P * b : P * (b + 1), :])
+
+        w_codes = []
+        w_scales = []
+        for o in range(PASSES):
+            grouped = keep.tile([P, N * PACK], BF16, name="grouped%d" % o, align_bytes=64)
+            nc.scalar.copy(
+                grouped[:].rearrange("p (c i t) -> p c t i", i=4, t=PACK),
+                w_raw[o][:].rearrange("p t (c i) -> p c t i", i=4),
+            )
+            codes = keep.tile([P, N], U32, name="w_codes%d" % o, align_bytes=64)
+            scales = keep.tile([P, N], U8, name="w_scales%d" % o, align_bytes=64)
+            nc.vector.quantize_mx(out=codes[:].bitcast(FP8X4), scales=scales[:], in_=grouped[:])
+            w_codes.append(codes)
+            w_scales.append(scales)
+
+        x_bytes = keep.tile([P, S], U8, name="x_bytes", align_bytes=64)
+        nc.vector.tensor_copy(x_bytes[:], scale_table[:].indirect(offsets[:]))
+        x_codes = [keep.tile([P, S], U32, name="x_codes%d" % o, align_bytes=64) for o in range(PASSES)]
+
+        def gather(o, lo, hi):
+            nc.vector.tensor_copy(
+                x_codes[o][:, lo:hi], word_table[o][:].bitcast(U32).indirect(offsets[:, lo // 16 : hi // 16])
+            )
+
+        pieces = ((0, 0, H), (0, H, S), (1, 0, S))
+        y = {pc: psum.tile([P, pc[2] - pc[1]], F32, name="y%d_%d" % pc[:2]) for pc in pieces}
+
+        def product(o, pc):
+            b, lo, hi = pc
+            cols = slice(P * b, P * (b + 1))
+            nc.tensor.matmul_mx(
+                out=y[pc][:],
+                lhsT=w_codes[o][:, cols].bitcast(FP8X4),
+                lhsT_scale=w_scales[o][:, cols],
+                rhs=x_codes[o][:, lo:hi].bitcast(FP8X4),
+                rhs_scale=x_bytes[4 * o : P, lo:hi],
+                start=(o == 0),
+                stop=(o == PASSES - 1),
+            )
+
+        gather(0, 0, S)
+        for pc in pieces:
+            product(0, pc)
+        gather(1, 0, H)
+        product(1, pieces[0])
+        gather(1, H, S)
+        product(1, pieces[1])
+        product(1, pieces[2])
+
+        p1 = [keep.tile([P, S], F32, name="p1_%d" % b, align_bytes=64) for b in range(ROW_TILES)]
+        u = [keep.tile([P, S], F32, name="u%d" % b, align_bytes=64) for b in range(ROW_TILES)]
+        ds = [keep.tile([P, S], F32, name="ds%d" % b, align_bytes=64) for b in range(ROW_TILES)]
+        acc = [keep.tile([P, S], F32, name="acc%d" % b, align_bytes=64) for b in range(ROW_TILES)]
+        res = [keep.tile([P, S], F32, name="res%d" % b, align_bytes=64) for b in range(ROW_TILES)]
+
+        def op_ds(b):
+            nc.scalar.activation(ds[b][:], data_sb[b][:], ACT.Copy, scale=C_DATA)
+
+        def op_t(pc):
+            b, lo, hi = pc
+            nc.vector.scalar_tensor_tensor(p1[b][:, lo:hi], y[pc][:], -STEP, dual_sb[b][:, lo:hi], ALU.mult, ALU.add)
+
+        def op_p(pc):
+            b, lo, hi = pc
+            first = max(lo, 1)
+            dst = p1[b][:, first - 1 : hi - 1]
+            nc.vector.scalar_tensor_tensor(dst, y[pc][:, first - lo :], STEP, dst, ALU.mult, ALU.add)
+
+        def op_r(b, lo, hi):
+            nc.scalar.activation(r[b][:, PAD + lo : PAD + hi], p1[b][:, lo:hi], ACT.Relu, bias=C_DIV, scale=-C_DIV)
+
+        def op_u(pc):
+            b, lo, hi = pc
+            nc.vector.scalar_tensor_tensor(u[b][:, lo:hi], y[pc][:], C_Y, ds[b][:, lo:hi], ALU.mult, ALU.add)
+
+        def op_w(b, lo, hi):
+            nc.vector.scalar_tensor_tensor(
+                acc[b][:, lo:hi], r[b][:, PAD + lo : PAD + hi], 2 * C_DIV, u[b][:, lo:hi], ALU.min, ALU.subtract
+            )
+
+        def op_o(b, lo, hi):
+            nc.vector.scalar_tensor_tensor(
+                res[b][:, lo:hi], r[b][:, PAD - 1 + lo : PAD - 1 + hi], 2 * C_DIV, acc[b][:, lo:hi], ALU.min, ALU.subtract
+            )
+            nc.sync.dma_start(out[P * b : P * (b + 1), lo:hi], res[b][:, lo:hi])
+
+        left, right, second = pieces
+        op_ds(0)
+        op_u(left)
+        op_t(left)
+        op_t(right)
+        op_p(left)
+        op_r(0, 0, H - 1)
+        op_u(right)
+        op_p(right)
+        op_r(0, H - 1, S)
+        op_ds(1)
+        op_t(second)
+        op_w(0, 0, S)
+        op_p(second)
+        op_r(1, 0, S)
+        op_o(0, 0, S)
+        op_u(second)
+        op_w(1, 0, H)
+        op_w(1, H, S)
+        op_o(1, 0, H)
+        op_o(1, H, S)

@@ -86,7 +86,7 @@ def tile_picked_ytvpd_step_p_kernel(tc, x_words, x_scales, w1, dual, data, offs,
                 x_codes[o][:, lo:hi], word_table[o][:].bitcast(U32).indirect(offsets[:, lo // 16 : hi // 16])
             )
 
-        pieces = ((0, 0, H), (0, H, S), (1, 0, S))
+        pieces = ((0, 0, H), (1, 0, H), (0, H, S), (1, H, S))
         y = {pc: psum.tile([P, pc[2] - pc[1]], F32, name="y%d_%d" % pc[:2]) for pc in pieces}
 
         def product(o, pc):
@@ -107,9 +107,10 @@ def tile_picked_ytvpd_step_p_kernel(tc, x_words, x_scales, w1, dual, data, offs,
             product(0, pc)
         gather(1, 0, H)
         product(1, pieces[0])
-        gather(1, H, S)
         product(1, pieces[1])
+        gather(1, H, S)
         product(1, pieces[2])
+        product(1, pieces[3])
 
         p1 = [keep.tile([P, S], F32, name="p1_%d" % b, align_bytes=64) for b in range(ROW_TILES)]
         u = [keep.tile([P, S], F32, name="u%d" % b, align_bytes=64) for b in range(ROW_TILES)]
@@ -148,23 +149,32 @@ def tile_picked_ytvpd_step_p_kernel(tc, x_words, x_scales, w1, dual, data, offs,
             )
             nc.sync.dma_start(out[P * b : P * (b + 1), lo:hi], res[b][:, lo:hi])
 
-        left, right, second = pieces
+        ya = keep.tile([P, S], F32, name="ya", align_bytes=64)
+
+        def op_t_pool(pc):
+            b, lo, hi = pc
+            nc.scalar.activation(ya[:, lo:hi], y[pc][:], ACT.Copy, scale=STEP)
+            nc.gpsimd.tensor_tensor(p1[b][:, lo:hi], dual_sb[b][:, lo:hi], ya[:, lo:hi], ALU.subtract)
+
+        left0, left1, right0, right1 = pieces
         op_ds(0)
-        op_u(left)
-        op_t(left)
-        op_t(right)
-        op_p(left)
-        op_r(0, 0, H - 1)
-        op_u(right)
-        op_p(right)
-        op_r(0, H - 1, S)
+        op_u(left0)
+        op_t(left0)
+        op_t_pool(left1)
+        op_t(right0)
+        op_t_pool(right1)
+        op_p(left0)
+        op_u(right0)
+        op_p(right0)
         op_ds(1)
-        op_t(second)
-        op_w(0, 0, S)
-        op_p(second)
+        op_r(0, 0, S)
+        op_p(left1)
+        op_u(left1)
+        op_p(right1)
         op_r(1, 0, S)
+        op_w(0, 0, S)
+        op_u(right1)
         op_o(0, 0, S)
-        op_u(second)
         op_w(1, 0, H)
         op_w(1, H, S)
         op_o(1, 0, H)

@@ -33,11 +33,16 @@ def tile_picked_ytvpd_step_p_kernel(tc, x_words, x_scales, w1, dual, data, offs,
         keep = ctx.enter_context(tc.tile_pool(name="keep", bufs=1))
         psum = ctx.enter_context(tc.psum_pool(name="psum", bufs=1))
 
+        scale_table = keep.tile([P, PASSES * T], U8, name="scale_table", align_bytes=64)
+        nc.vector.memset(scale_table[: P - 16, :].bitcast(I32), 0)
+        nc.sync.dma_start(
+            scale_table[P - 16 :, :].bitcast(I32).rearrange("q (o c) -> q o c", o=PASSES),
+            x_scales.bitcast(I32).rearrange("o q c -> q o c"),
+        )
         offsets = keep.tile([P, S // 16], U16, name="offsets")
         nc.sync.dma_start(offsets[:], offs)
-
-        scale_table = keep.tile([P, T], U8, name="scale_table", align_bytes=64)
-        nc.gpsimd.memset(scale_table[:].bitcast(I32), 0)
+        x_bytes = keep.tile([P, PASSES * S], U8, name="x_bytes", align_bytes=64)
+        nc.gpsimd.memset(x_bytes[:].bitcast(I32), 0)
         zero = keep.tile([P, 1], F32, name="zero")
         nc.vector.memset(zero[:], 0.0)
 
@@ -48,26 +53,32 @@ def tile_picked_ytvpd_step_p_kernel(tc, x_words, x_scales, w1, dual, data, offs,
         w_raw = [keep.tile([P, PACK, N], F32, name="w_raw%d" % o, align_bytes=64) for o in range(PASSES)]
         for o in range(PASSES):
             nc.sync.dma_start(w_raw[o][:], w1[512 * o : 512 * (o + 1), :].rearrange("(p j) n -> p j n", j=PACK))
-            if o == 0:
-                for q in range(4):
-                    nc.sync.dma_start(
-                        scale_table[32 * q : 32 * q + 4 * PASSES, :].bitcast(I32),
-                        x_scales[:, 4 * q : 4 * q + 4, :].bitcast(I32),
-                    )
-
         word_table = [keep.tile([P, T], I32, name="word_table%d" % o, align_bytes=64) for o in range(PASSES)]
         for o in range(PASSES):
             nc.sync.dma_start(word_table[o][:], x_words[o].rearrange("p c r -> p (c r)").bitcast(I32))
-        dual_sb = [keep.tile([P, S], F32, name="dual%d" % b, align_bytes=64) for b in range(ROW_TILES)]
-        data_sb = [keep.tile([P, S], F32, name="data%d" % b, align_bytes=64) for b in range(ROW_TILES)]
-        for sb, src, b in ((data_sb, data, 0), (dual_sb, dual, 0), (dual_sb, dual, 1), (data_sb, data, 1)):
-            nc.sync.dma_start(sb[b][:], src[P * b : P * (b + 1), :])
+        dual_all = keep.tile([P, ROW_TILES, S], F32, name="dual_all", align_bytes=64)
+        data_all = keep.tile([P, ROW_TILES, S], F32, name="data_all", align_bytes=64)
+        nc.sync.dma_start(dual_all[:], dual.rearrange("(b p) j -> p b j", p=P))
+        nc.sync.dma_start(data_all[:], data.rearrange("(b p) j -> p b j", p=P))
+        dual_sb = [dual_all[:, b, :] for b in range(ROW_TILES)]
+        data_sb = [data_all[:, b, :] for b in range(ROW_TILES)]
+
+        picked_rows = keep.tile([P, PASSES * S], U8, name="picked_rows", align_bytes=64)
+        for o in range(PASSES):
+            nc.vector.tensor_copy(
+                picked_rows[:, S * o : S * (o + 1)], scale_table[:, T * o : T * (o + 1)].indirect(offsets[:])
+            )
+        for q in range(4):
+            first = P - 16 + 4 * q
+            nc.scalar.dma_start(
+                x_bytes[32 * q : 32 * q + 4, :].bitcast(I32), picked_rows[first : first + 4, :].bitcast(I32)
+            )
 
         w_codes = []
         w_scales = []
         for o in range(PASSES):
             grouped = keep.tile([P, N * PACK], BF16, name="grouped%d" % o, align_bytes=64)
-            nc.scalar.copy(
+            (nc.scalar.copy, nc.vector.tensor_copy)[o](
                 grouped[:].rearrange("p (c i t) -> p c t i", i=4, t=PACK),
                 w_raw[o][:].rearrange("p t (c i) -> p c t i", i=4),
             )
@@ -77,8 +88,6 @@ def tile_picked_ytvpd_step_p_kernel(tc, x_words, x_scales, w1, dual, data, offs,
             w_codes.append(codes)
             w_scales.append(scales)
 
-        x_bytes = keep.tile([P, S], U8, name="x_bytes", align_bytes=64)
-        nc.vector.tensor_copy(x_bytes[:], scale_table[:].indirect(offsets[:]))
         x_codes = [keep.tile([P, S], U32, name="x_codes%d" % o, align_bytes=64) for o in range(PASSES)]
 
         def gather(o, lo, hi):
@@ -97,7 +106,7 @@ def tile_picked_ytvpd_step_p_kernel(tc, x_words, x_scales, w1, dual, data, offs,
                 lhsT=w_codes[o][:, cols].bitcast(FP8X4),
                 lhsT_scale=w_scales[o][:, cols],
                 rhs=x_codes[o][:, lo:hi].bitcast(FP8X4),
-                rhs_scale=x_bytes[4 * o : P, lo:hi],
+                rhs_scale=x_bytes[:, S * o + lo : S * o + hi],
                 start=(o == 0),
                 stop=(o == PASSES - 1),
             )
@@ -119,7 +128,7 @@ def tile_picked_ytvpd_step_p_kernel(tc, x_words, x_scales, w1, dual, data, offs,
         res = [keep.tile([P, S], F32, name="res%d" % b, align_bytes=64) for b in range(ROW_TILES)]
 
         def op_ds(b):
-            nc.scalar.activation(ds[b][:], data_sb[b][:], ACT.Copy, scale=C_DATA)
+            nc.scalar.activation(ds[b][:], data_sb[b], ACT.Copy, scale=C_DATA)
 
         def op_t(pc):
             b, lo, hi = pc
@@ -157,22 +166,22 @@ def tile_picked_ytvpd_step_p_kernel(tc, x_words, x_scales, w1, dual, data, offs,
             nc.gpsimd.tensor_tensor(p1[b][:, lo:hi], dual_sb[b][:, lo:hi], ya[:, lo:hi], ALU.subtract)
 
         left0, left1, right0, right1 = pieces
-        op_ds(0)
-        op_u(left0)
         op_t(left0)
-        op_t_pool(left1)
+        op_t(left1)
         op_t(right0)
         op_t_pool(right1)
         op_p(left0)
-        op_u(right0)
-        op_p(right0)
-        op_ds(1)
-        op_r(0, 0, S)
         op_p(left1)
-        op_u(left1)
+        op_p(right0)
+        op_ds(0)
+        op_r(0, 0, S)
+        op_u(left0)
+        op_u(right0)
         op_p(right1)
+        op_ds(1)
         op_r(1, 0, S)
         op_w(0, 0, S)
+        op_u(left1)
         op_u(right1)
         op_o(0, 0, S)
         op_w(1, 0, H)

@@ -31,9 +31,10 @@ def tile_picked_ytvpd_step_p_kernel(tc, x_words, x_scales, w1, dual, data, offs,
     nc = tc.nc
     with ExitStack() as ctx:
         keep = ctx.enter_context(tc.tile_pool(name="keep", bufs=1))
+        reuse = ctx.enter_context(tc.tile_pool(name="reuse", bufs=1))
         psum = ctx.enter_context(tc.psum_pool(name="psum", bufs=1))
 
-        scale_table = keep.tile([P, PASSES * T], U8, name="scale_table", align_bytes=64)
+        scale_table = reuse.tile([P, PASSES * T], U8, name="scale_table", align_bytes=64, offset=16 * S - T)
         nc.vector.memset(scale_table[: P - 16, :].bitcast(I32), 0)
         nc.sync.dma_start(
             scale_table[P - 16 :, :].bitcast(I32).rearrange("q (o c) -> q o c", o=PASSES),
@@ -50,19 +51,16 @@ def tile_picked_ytvpd_step_p_kernel(tc, x_words, x_scales, w1, dual, data, offs,
         for b in range(ROW_TILES):
             nc.scalar.activation(r[b][:, PAD - 1 : PAD], zero[:], ACT.Relu, bias=C_DIV, scale=1.0)
 
-        w_raw = [keep.tile([P, PACK, N], F32, name="w_raw%d" % o, align_bytes=64) for o in range(PASSES)]
-        for o in range(PASSES):
-            nc.sync.dma_start(w_raw[o][:], w1[512 * o : 512 * (o + 1), :].rearrange("(p j) n -> p j n", j=PACK))
+        w_raw = {}
+
+        def load_w(o, tile):
+            w_raw[o] = tile
+            nc.sync.dma_start(tile[:], w1[512 * o : 512 * (o + 1), :].rearrange("(p j) n -> p j n", j=PACK))
+
+        load_w(0, keep.tile([P, PACK, N], F32, name="w_raw0", align_bytes=64))
         word_table = [keep.tile([P, T], I32, name="word_table%d" % o, align_bytes=64) for o in range(PASSES)]
         for o in range(PASSES):
             nc.sync.dma_start(word_table[o][:], x_words[o].rearrange("p c r -> p (c r)").bitcast(I32))
-        dual_all = keep.tile([P, ROW_TILES, S], F32, name="dual_all", align_bytes=64)
-        data_all = keep.tile([P, ROW_TILES, S], F32, name="data_all", align_bytes=64)
-        nc.sync.dma_start(dual_all[:], dual.rearrange("(b p) j -> p b j", p=P))
-        nc.sync.dma_start(data_all[:], data.rearrange("(b p) j -> p b j", p=P))
-        dual_sb = [dual_all[:, b, :] for b in range(ROW_TILES)]
-        data_sb = [data_all[:, b, :] for b in range(ROW_TILES)]
-
         picked_rows = keep.tile([P, PASSES * S], U8, name="picked_rows", align_bytes=64)
         for o in range(PASSES):
             nc.vector.tensor_copy(
@@ -70,24 +68,35 @@ def tile_picked_ytvpd_step_p_kernel(tc, x_words, x_scales, w1, dual, data, offs,
             )
         for q in range(4):
             first = P - 16 + 4 * q
-            nc.scalar.dma_start(
+            nc.sync.dma_start(
                 x_bytes[32 * q : 32 * q + 4, :].bitcast(I32), picked_rows[first : first + 4, :].bitcast(I32)
             )
 
-        w_codes = []
-        w_scales = []
-        for o in range(PASSES):
-            grouped = keep.tile([P, N * PACK], BF16, name="grouped%d" % o, align_bytes=64)
-            (nc.scalar.copy, nc.vector.tensor_copy)[o](
-                grouped[:].rearrange("p (c i t) -> p c t i", i=4, t=PACK),
-                w_raw[o][:].rearrange("p t (c i) -> p c t i", i=4),
-            )
-            codes = keep.tile([P, N], U32, name="w_codes%d" % o, align_bytes=64)
-            scales = keep.tile([P, N], U8, name="w_scales%d" % o, align_bytes=64)
-            nc.vector.quantize_mx(out=codes[:].bitcast(FP8X4), scales=scales[:], in_=grouped[:])
-            w_codes.append(codes)
-            w_scales.append(scales)
+        load_w(1, reuse.tile([P, PACK, N], F32, name="w_raw1", align_bytes=64, offset=16 * S))
+        late = reuse.tile([P, 2 * ROW_TILES, S], F32, name="late", align_bytes=64, offset=0)
+        dual_sb = [late[:, b, :] for b in range(ROW_TILES)]
+        data_sb = [late[:, ROW_TILES + b, :] for b in range(ROW_TILES)]
+        for sb, src, b in ((data_sb, data, 0), (dual_sb, dual, 0), (dual_sb, dual, 1), (data_sb, data, 1)):
+            nc.sync.dma_start(sb[b], src[P * b : P * (b + 1), :])
 
+        w_codes = {}
+        w_scales = {}
+
+        def quantise(o, lo, hi, copy):
+            width = hi - lo
+            grouped = keep.tile([P, width * PACK], BF16, name="grouped%d_%d" % (o, lo), align_bytes=64)
+            copy(
+                grouped[:].rearrange("p (c i t) -> p c t i", i=4, t=PACK),
+                w_raw[o][:, :, lo:hi].rearrange("p t (c i) -> p c t i", i=4),
+            )
+            codes = keep.tile([P, width], U32, name="w_codes%d_%d" % (o, lo), align_bytes=64)
+            scales = keep.tile([P, width], U8, name="w_scales%d_%d" % (o, lo), align_bytes=64)
+            nc.vector.quantize_mx(out=codes[:].bitcast(FP8X4), scales=scales[:], in_=grouped[:])
+            for b in range(lo // P, hi // P):
+                w_codes[o, b] = codes[:, P * b - lo : P * (b + 1) - lo]
+                w_scales[o, b] = scales[:, P * b - lo : P * (b + 1) - lo]
+
+        quantise(0, 0, N, nc.scalar.copy)
         x_codes = [keep.tile([P, S], U32, name="x_codes%d" % o, align_bytes=64) for o in range(PASSES)]
 
         def gather(o, lo, hi):
@@ -100,11 +109,10 @@ def tile_picked_ytvpd_step_p_kernel(tc, x_words, x_scales, w1, dual, data, offs,
 
         def product(o, pc):
             b, lo, hi = pc
-            cols = slice(P * b, P * (b + 1))
             nc.tensor.matmul_mx(
                 out=y[pc][:],
-                lhsT=w_codes[o][:, cols].bitcast(FP8X4),
-                lhsT_scale=w_scales[o][:, cols],
+                lhsT=w_codes[o, b].bitcast(FP8X4),
+                lhsT_scale=w_scales[o, b],
                 rhs=x_codes[o][:, lo:hi].bitcast(FP8X4),
                 rhs_scale=x_bytes[:, S * o + lo : S * o + hi],
                 start=(o == 0),
@@ -114,12 +122,11 @@ def tile_picked_ytvpd_step_p_kernel(tc, x_words, x_scales, w1, dual, data, offs,
         gather(0, 0, S)
         for pc in pieces:
             product(0, pc)
-        gather(1, 0, H)
-        product(1, pieces[0])
-        product(1, pieces[1])
-        gather(1, H, S)
-        product(1, pieces[2])
-        product(1, pieces[3])
+        gather(1, 0, S)
+        quantise(1, 0, P, nc.vector.tensor_copy)
+        quantise(1, P, N, nc.scalar.copy)
+        for pc in sorted(pieces):
+            product(1, pc)
 
         p1 = [keep.tile([P, S], F32, name="p1_%d" % b, align_bytes=64) for b in range(ROW_TILES)]
         u = [keep.tile([P, S], F32, name="u%d" % b, align_bytes=64) for b in range(ROW_TILES)]
@@ -166,22 +173,22 @@ def tile_picked_ytvpd_step_p_kernel(tc, x_words, x_scales, w1, dual, data, offs,
             nc.gpsimd.tensor_tensor(p1[b][:, lo:hi], dual_sb[b][:, lo:hi], ya[:, lo:hi], ALU.subtract)
 
         left0, left1, right0, right1 = pieces
+        op_ds(0)
+        op_u(left0)
         op_t(left0)
-        op_t(left1)
+        op_t_pool(left1)
         op_t(right0)
         op_t_pool(right1)
         op_p(left0)
-        op_p(left1)
-        op_p(right0)
-        op_ds(0)
-        op_r(0, 0, S)
-        op_u(left0)
         op_u(right0)
-        op_p(right1)
+        op_p(right0)
         op_ds(1)
+        op_r(0, 0, S)
+        op_p(left1)
+        op_u(left1)
+        op_p(right1)
         op_r(1, 0, S)
         op_w(0, 0, S)
-        op_u(left1)
         op_u(right1)
         op_o(0, 0, S)
         op_w(1, 0, H)

from contextlib import ExitStack

import concourse.mybir as mybir

K, T, S, N = 1024, 2048, 512, 256
FLOPS = 2 * K * S * N

F32 = mybir.dt.float32
BF16 = mybir.dt.bfloat16
I32 = mybir.dt.int32
U32 = mybir.dt.uint32
U16 = mybir.dt.uint16
U8 = mybir.dt.uint8
FP8X4 = mybir.dt.float8_e4m3fn_x4
ALU = mybir.AluOpType
ACT = mybir.ActivationFunctionType

P = 128
PACK = 4
PASSES = K // (P * PACK)
ROW_TILES = N // P
STEP = 0.4
C_DIV = 0.4 / 1.8
C_Y = 1.0 / 1.8
C_DATA = 0.8 / 1.8
PAD = 8
H = S // 2


def tile_picked_ytvpd_step_p_kernel(tc, x_words, x_scales, w1, dual, data, offs, out):
    nc = tc.nc
    with ExitStack() as ctx:
        keep = ctx.enter_context(tc.tile_pool(name="keep", bufs=1))
        reuse = ctx.enter_context(tc.tile_pool(name="reuse", bufs=1))
        psum = ctx.enter_context(tc.psum_pool(name="psum", bufs=1))

        scale_table = reuse.tile([P, PASSES * T], U8, name="scale_table", align_bytes=64, offset=16 * S - T)
        nc.vector.memset(scale_table[: P - 16, :].bitcast(I32), 0)
        nc.sync.dma_start(
            scale_table[P - 16 :, :].bitcast(I32).rearrange("q (o c) -> q o c", o=PASSES),
            x_scales.bitcast(I32).rearrange("o q c -> q o c"),
        )
        offsets = keep.tile([P, S // 16], U16, name="offsets")
        nc.sync.dma_start(offsets[:], offs)
        x_bytes = keep.tile([P, PASSES * S], U8, name="x_bytes", align_bytes=64)
        nc.gpsimd.memset(x_bytes[:].bitcast(I32), 0)
        zero = keep.tile([P, 1], F32, name="zero")
        nc.vector.memset(zero[:], 0.0)

        r = [keep.tile([P, PAD + S], F32, name="r%d" % b, align_bytes=64) for b in range(ROW_TILES)]
        for b in range(ROW_TILES):
            nc.scalar.activation(r[b][:, PAD - 1 : PAD], zero[:], ACT.Relu, bias=C_DIV, scale=1.0)

        w_raw = {}

        def load_w(o, tile):
            w_raw[o] = tile
            nc.sync.dma_start(tile[:], w1[512 * o : 512 * (o + 1), :].rearrange("(p j) n -> p j n", j=PACK))

        load_w(0, keep.tile([P, PACK, N], F32, name="w_raw0", align_bytes=64))
        word_table = [keep.tile([P, T], I32, name="word_table%d" % o, align_bytes=64) for o in range(PASSES)]
        for o in range(PASSES):
            nc.sync.dma_start(word_table[o][:], x_words[o].rearrange("p c r -> p (c r)").bitcast(I32))
        picked_rows = keep.tile([P, PASSES * S], U8, name="picked_rows", align_bytes=64)
        for o in range(PASSES):
            nc.vector.tensor_copy(
                picked_rows[:, S * o : S * (o + 1)], scale_table[:, T * o : T * (o + 1)].indirect(offsets[:])
            )
        for q in range(4):
            first = P - 16 + 4 * q
            nc.sync.dma_start(
                x_bytes[32 * q : 32 * q + 4, :].bitcast(I32), picked_rows[first : first + 4, :].bitcast(I32)
            )

        load_w(1, reuse.tile([P, PACK, N], F32, name="w_raw1", align_bytes=64, offset=16 * S))
        late = reuse.tile([P, 2 * ROW_TILES, S], F32, name="late", align_bytes=64, offset=0)
        dual_sb = [late[:, b, :] for b in range(ROW_TILES)]
        data_sb = [late[:, ROW_TILES + b, :] for b in range(ROW_TILES)]
        for sb, src, b in ((data_sb, data, 0), (dual_sb, dual, 0), (dual_sb, dual, 1), (data_sb, data, 1)):
            nc.sync.dma_start(sb[b], src[P * b : P * (b + 1), :])

        w_codes = {}
        w_scales = {}

        def quantise(o, lo, hi, copy):
            width = hi - lo
            grouped = keep.tile([P, width * PACK], BF16, name="grouped%d_%d" % (o, lo), align_bytes=64)
            copy(
                grouped[:].rearrange("p (c i t) -> p c t i", i=4, t=PACK),
                w_raw[o][:, :, lo:hi].rearrange("p t (c i) -> p c t i", i=4),
            )
            codes = keep.tile([P, width], U32, name="w_codes%d_%d" % (o, lo), align_bytes=64)
            scales = keep.tile([P, width], U8, name="w_scales%d_%d" % (o, lo), align_bytes=64)
            nc.vector.quantize_mx(out=codes[:].bitcast(FP8X4), scales=scales[:], in_=grouped[:])
            for b in range(lo // P, hi // P):
                w_codes[o, b] = codes[:, P * b - lo : P * (b + 1) - lo]
                w_scales[o, b] = scales[:, P * b - lo : P * (b + 1) - lo]

        quantise(0, 0, N, nc.scalar.copy)
        x_codes = [keep.tile([P, S], U32, name="x_codes%d" % o, align_bytes=64) for o in range(PASSES)]

        def gather(o, lo, hi):
            nc.vector.tensor_copy(
                x_codes[o][:, lo:hi], word_table[o][:].bitcast(U32).indirect(offsets[:, lo // 16 : hi // 16])
            )

        pieces = ((0, 0, H), (1, 0, H), (0, H, S), (1, H, S))
        y = {pc: psum.tile([P, pc[2] - pc[1]], F32, name="y%d_%d" % pc[:2]) for pc in pieces}

        def product(o, pc):
            b, lo, hi = pc
            nc.tensor.matmul_mx(
                out=y[pc][:],
                lhsT=w_codes[o, b].bitcast(FP8X4),
                lhsT_scale=w_scales[o, b],
                rhs=x_codes[o][:, lo:hi].bitcast(FP8X4),
                rhs_scale=x_bytes[:, S * o + lo : S * o + hi],
                start=(o == 0),
                stop=(o == PASSES - 1),
            )

        gather(0, 0, S)
        for pc in pieces:
            product(0, pc)
        gather(1, 0, S)
        quantise(1, 0, P, nc.vector.tensor_copy)
        quantise(1, P, N, nc.scalar.copy)
        for pc in sorted(pieces):
            product(1, pc)

        p1 = [keep.tile([P, S], F32, name="p1_%d" % b, align_bytes=64) for b in range(ROW_TILES)]
        u = [keep.tile([P, S], F32, name="u%d" % b, align_bytes=64) for b in range(ROW_TILES)]
        ds = [keep.tile([P, S], F32, name="ds%d" % b, align_bytes=64) for b in range(ROW_TILES)]
        acc = [keep.tile([P, S], F32, name="acc%d" % b, align_bytes=64) for b in range(ROW_TILES)]
        res = [keep.tile([P, S], F32, name="res%d" % b, align_bytes=64) for b in range(ROW_TILES)]

        def op_ds(b):
            nc.scalar.activation(ds[b][:], data_sb[b], ACT.Copy, scale=C_DATA)

        def op_t(pc):
            b, lo, hi = pc
            nc.vector.scalar_tensor_tensor(p1[b][:, lo:hi], y[pc][:], -STEP, dual_sb[b][:, lo:hi], ALU.mult, ALU.add)

        def op_p(pc):
            b, lo, hi = pc
            first = max(lo, 1)
            dst = p1[b][:, first - 1 : hi - 1]
            nc.vector.scalar_tensor_tensor(dst, y[pc][:, first - lo :], STEP, dst, ALU.mult, ALU.add)

        def op_r(b, lo, hi):
            nc.scalar.activation(r[b][:, PAD + lo : PAD + hi], p1[b][:, lo:hi], ACT.Relu, bias=C_DIV, scale=-C_DIV)

        def op_u(pc):
            b, lo, hi = pc
            nc.vector.scalar_tensor_tensor(u[b][:, lo:hi], y[pc][:], C_Y, ds[b][:, lo:hi], ALU.mult, ALU.add)

        def op_w(b, lo, hi):
            nc.vector.scalar_tensor_tensor(
                acc[b][:, lo:hi], r[b][:, PAD + lo : PAD + hi], 2 * C_DIV, u[b][:, lo:hi], ALU.min, ALU.subtract
            )

        def op_o(b, lo, hi):
            nc.vector.scalar_tensor_tensor(
                res[b][:, lo:hi], r[b][:, PAD - 1 + lo : PAD - 1 + hi], 2 * C_DIV, acc[b][:, lo:hi], ALU.min, ALU.subtract
            )
            nc.sync.dma_start(out[P * b : P * (b + 1), lo:hi], res[b][:, lo:hi])

        ya = keep.tile([P, S], F32, name="ya", align_bytes=64)

        def op_t_pool(pc):
            b, lo, hi = pc
            nc.scalar.activation(ya[:, lo:hi], y[pc][:], ACT.Copy, scale=STEP)
            nc.gpsimd.tensor_tensor(p1[b][:, lo:hi], dual_sb[b][:, lo:hi], ya[:, lo:hi], ALU.subtract)

        left0, left1, right0, right1 = pieces
        op_ds(0)
        op_u(left0)
        op_t(left0)
        op_t_pool(left1)
        op_t(right0)
        op_t_pool(right1)
        op_p(left0)
        op_u(right0)
        op_p(right0)
        op_ds(1)
        op_r(0, 0, S)
        op_p(left1)
        op_u(left1)
        op_p(right1)
        op_r(1, 0, S)
        op_w(0, 0, S)
        op_u(right1)
        op_o(0, 0, S)
        op_w(1, 0, H)
        op_w(1, H, S)
        op_o(1, 0, H)
        op_o(1, H, S)
